import numpy as np
import ml_dtypes


def mxq(x, axis, fmt="e4m3"):
    dtype, down = {"e4m3": (ml_dtypes.float8_e4m3fn, 7), "e5m2": (ml_dtypes.float8_e5m2, 14)}[fmt]
    v = np.moveaxis(np.asarray(x, np.float32).astype(ml_dtypes.bfloat16).astype(np.float64), axis, -1)
    blocks = v.reshape(v.shape[:-1] + (-1, 32))
    amax = np.abs(blocks).max(-1, keepdims=True)
    byte = np.maximum(np.where(amax > 0, np.frexp(amax)[1] - 1 + 127, 0) - down, 1)
    scale = np.exp2(byte - 127.0)
    codes = (blocks / scale).astype(np.float32).astype(dtype).astype(np.float64)
    return np.moveaxis((codes * scale).reshape(v.shape), -1, axis)


WIDE = False


def mx_kscale(k):
    if not WIDE:
        return np.ones(k)
    levels = np.array([10, -10, 5, -5, 0])
    if k % 512:
        return np.exp2(np.random.permutation(np.resize(levels, k // 32))).repeat(32)
    a = np.empty((k // 512, 16))
    for p in range(k // 512):
        a[p, :8] = np.random.permutation(np.resize(levels, 8))
        for g in range(8):
            far = levels[np.abs(levels - a[p, g]) >= 10]
            a[p, g + 8] = far[np.random.randint(len(far))]
    return np.exp2(a.ravel()).repeat(32)


def f64(x):
    return np.asarray(x).astype(np.float64)


def striped(idx):
    return np.tile(idx.reshape(-1, 16).T, (8, 1)).astype(np.uint16)


def unstriped(offs):
    return offs[:16].T.reshape(-1).astype(np.int64)


def striped8(idx):
    return np.concatenate([x.reshape(-1, 16).T for x in idx]).astype(np.uint16)


def runs(offs, k):
    lists = np.stack([offs[16 * r : 16 * r + 16].T.reshape(-1) for r in range(8)]).astype(np.int64)
    return lists[np.arange(k) % 512 // 64]


def pack_weight(w):
    k, n = w.shape
    w = f64(np.asarray(w, np.float32).astype(ml_dtypes.bfloat16)).reshape(k // 32, 32, n)
    amax = np.abs(w).max(1)
    byte = np.clip(np.where(amax > 0, np.frexp(amax)[1] - 1 + 127 - 7, 1), 1, 254)
    scaled = (w * np.exp2(127.0 - byte)[:, None, :]).reshape(k, n).astype(np.float32)
    words = np.ascontiguousarray(scaled.reshape(k // 512, 128, 4, n).transpose(0, 1, 3, 2)).astype(ml_dtypes.float8_e4m3fn).view(np.uint8)
    return words, np.ascontiguousarray(byte.astype(np.uint8).reshape(k // 512, 16, n))


def unpack_weight(words, scales):
    g, p, n, _ = words.shape
    vals = np.ascontiguousarray(words).view(ml_dtypes.float8_e4m3fn).astype(np.float64) * np.repeat(np.exp2(scales.astype(np.float64) - 127.0), 8, axis=1)[..., None]
    return vals.transpose(0, 1, 3, 2).reshape(g * 512, n)


E2M1 = np.array([0.0, 0.5, 1.0, 1.5, 2.0, 3.0, 4.0, 6.0, -0.0, -0.5, -1.0, -1.5, -2.0, -3.0, -4.0, -6.0])


def pack_fp4(w):
    k, n = w.shape
    w = f64(np.asarray(w, np.float32).astype(ml_dtypes.bfloat16)).reshape(k // 32, 32, n)
    amax = np.abs(w).max(1)
    mant, ex = np.frexp(amax / 6.0)
    byte = np.clip(np.where(amax > 0, np.where(mant > 0.5, ex, ex - 1) + 127, 1), 1, 254)
    scaled = (w * np.exp2(127.0 - byte)[:, None, :]).reshape(k, n).astype(np.float32)
    c = np.ascontiguousarray(scaled.reshape(k // 512, 128, 4, n).transpose(0, 1, 3, 2)).astype(ml_dtypes.float4_e2m1fn).view(np.uint8) & 0xF
    words = (c[..., 0::2] | (c[..., 1::2] << 4)).reshape(k // 512, 128, 2 * n)
    return np.ascontiguousarray(words), np.ascontiguousarray(byte.astype(np.uint8).reshape(k // 512, 16, n))


def unpack_fp4(words, scales):
    g, _, n = scales.shape
    words = np.ascontiguousarray(words).reshape(g, 128, n, 2)
    nib = np.empty((g, 128, n, 4), np.uint8)
    nib[..., 0::2] = words & 0xF
    nib[..., 1::2] = words >> 4
    vals = E2M1[nib] * np.repeat(np.exp2(scales.astype(np.float64) - 127.0), 8, axis=1)[..., None]
    return vals.transpose(0, 1, 3, 2).reshape(g * 512, n)


K, T, S, N, G, H, W, U = 512, 2048, 256, 512, 2048, 512, 128, 512


def setup_inputs():
    n = np.random.standard_normal
    s = mx_kscale(K)[:, None]
    u = mx_kscale(K)
    packed_xT = pack_weight(n((K, T)) * s)
    packed_dT = pack_weight(n((K, G)) / s)
    packed_w1 = pack_fp4(n((H, N)) / np.sqrt(H) / u[:, None])
    perm = np.random.permutation(S)
    perm2 = np.random.permutation(U)
    return {
        "x_words": packed_xT[0],
        "x_scales": packed_xT[1],
        "d_words": packed_dT[0],
        "d_scales": packed_dT[1],
        "gn": (np.random.uniform(0.5, 1.5, (H, 1)) * u[:, None]).astype(np.float32),
        "w1_words": packed_w1[0],
        "w1_scales": packed_w1[1],
        "offs": striped(np.random.permutation(T)[:S]),
        "k1": striped8(np.random.randint(0, G, (8, H))),
        "n1": striped(perm[:W]),
        "n2": striped(perm[W:]),
        "n3": striped(np.random.permutation(S)),
        "n4": striped(perm2[:S]),
        "n5": striped(perm2[S:]),
        "n6": striped(np.random.permutation(S)),
    }


def reference(x_words, x_scales, d_words, d_scales, gn, w1_words, w1_scales, offs, k1, n1, n2, n3, n4, n5, n6):
    d_k1 = unpack_weight(d_words, d_scales)[np.arange(K)[:, None], runs(k1, K)]
    xq = unpack_weight(x_words, x_scales)[:, unstriped(offs)]
    h = 0.0625 * (d_k1.T @ xq)
    pa = h[:, unstriped(n1)]
    pb = h[:, unstriped(n2)]
    rb = pa - pb
    ds = np.zeros((H, S))
    ds[:, unstriped(n1)] = pb
    dt = ds.copy()
    dt[:, unstriped(n2)] = rb
    z = f64(gn) * (np.maximum(dt, 0.5 * dt[:, unstriped(n3)]))
    h2 = unpack_fp4(w1_words, w1_scales).T @ mxq(z, 0, "e4m3")
    nw = h2 - h2[:, unstriped(n6)]
    ph = np.zeros((N, U))
    ph[:, unstriped(n4)] = h2
    out = ph.copy()
    out[:, unstriped(n5)] = nw
    return out

@@ -1,0 +1,201 @@
+from contextlib import ExitStack
+
+import concourse.mybir as mybir
+
+F32 = mybir.dt.float32
+BF16 = mybir.dt.bfloat16
+I32 = mybir.dt.int32
+U32 = mybir.dt.uint32
+U16 = mybir.dt.uint16
+U8 = mybir.dt.uint8
+FP8X4 = mybir.dt.float8_e4m3fn_x4
+FP4X4 = mybir.dt.float4_e2m1fn_x4
+ALU = mybir.AluOpType
+COPY = mybir.ActivationFunctionType.Copy
+
+P = 128
+PACK = 4
+T = 2048
+S = 256
+H = 512
+W = 128
+U = 512
+SPARE = 8
+FLOPS = 2 * 512 * 512 * 256 * 2
+
+
+def tile_picked_pqlayswapdpagq_none_p_kernel(
+    tc, x_words, x_scales, d_words, d_scales, gn, w1_words, w1_scales, offs, k1, n1, n2, n3, n4, n5, n6, out
+):
+    nc = tc.nc
+    with ExitStack() as ctx:
+        lists = ctx.enter_context(tc.tile_pool(name="lists", bufs=1))
+        keep = ctx.enter_context(tc.tile_pool(name="keep", bufs=1))
+        psum = ctx.enter_context(tc.psum_pool(name="psum", bufs=4))
+
+        def load_list(src, name):
+            tile = lists.tile(list(src.shape), U16, name=name)
+            nc.sync.dma_start(tile[:], src)
+            return tile
+
+        d_scale_win = keep.tile([P, T], U8, name="d_scale_win", align_bytes=64)
+        x_scale_win = keep.tile([P, T], U8, name="x_scale_win", tag="shared", align_bytes=64)
+        placed = keep.tile([P, H + S], U8, name="placed", align_bytes=64)
+        w1_plane = keep.tile([P, H], U8, name="w1_plane", align_bytes=64)
+        nc.vector.memset(d_scale_win[:].bitcast(I32), 0)
+        nc.vector.memset(x_scale_win[:].bitcast(I32), 0)
+        nc.vector.memset(placed[:].bitcast(I32), 0)
+        nc.vector.memset(w1_plane[:].bitcast(I32), 0)
+
+        k1_sb = load_list(k1, "k1_sb")
+        offs_sb = load_list(offs, "offs_sb")
+        nc.scalar.dma_start(d_scale_win[:].bitcast(I32)[0:P:8, :], d_scales[0].bitcast(I32))
+        nc.scalar.dma_start(x_scale_win[:].bitcast(I32)[0:P:8, :], x_scales[0].bitcast(I32))
+        d_win = keep.tile([P, T], U32, name="d_win", align_bytes=64)
+        x_win = keep.tile([P, T], U32, name="x_win", align_bytes=64)
+        nc.sync.dma_start(d_win[:].bitcast(I32), d_words[0].rearrange("p n t -> p (n t)").bitcast(I32))
+        nc.gpsimd.dma_start(x_win[:].bitcast(I32), x_words[0].rearrange("p n t -> p (n t)").bitcast(I32))
+        n2_sb = load_list(n2, "n2_sb")
+        n1_sb = load_list(n1, "n1_sb")
+        n3_sb = load_list(n3, "n3_sb")
+        n4_sb = load_list(n4, "n4_sb")
+        n6_sb = load_list(n6, "n6_sb")
+        n5_sb = load_list(n5, "n5_sb")
+
+        gain = keep.tile([P, PACK], F32, name="gain")
+        nc.gpsimd.dma_start(gain[:], gn.rearrange("(p t) o -> p (t o)", t=PACK))
+        w1_sb = keep.tile([P, 2 * H], U8, name="w1_sb", align_bytes=64)
+        nc.gpsimd.dma_start(w1_sb[:].bitcast(I32), w1_words[0].bitcast(I32))
+        for q in range(4):
+            nc.gpsimd.dma_start(
+                w1_plane[:].bitcast(I32)[32 * q : 32 * q + 4, :], w1_scales[0].bitcast(I32)[4 * q : 4 * q + 4, :]
+            )
+
+        h2 = [keep.tile([P, S + SPARE], F32, name="h2_%d" % u) for u in range(4)]
+        for u in range(4):
+            nc.vector.memset(h2[u][:, S:], 0.0)
+
+        picked = keep.tile([P, H + S], U8, name="picked", align_bytes=64)
+        nc.vector.tensor_copy(picked[:, :H], d_scale_win[:].indirect(k1_sb[:]))
+        nc.vector.tensor_copy(picked[:, H:], x_scale_win[:].indirect(offs_sb[:]))
+        for a in range(4):
+            nc.scalar.dma_start(placed[:].bitcast(I32)[a:P:32, :], picked[:].bitcast(I32)[8 * a : P : 32, :])
+
+        d_picked = keep.tile([P, H], U32, name="d_picked", tag="shared", align_bytes=64)
+        nc.vector.tensor_copy(d_picked[:], d_win[:].indirect(k1_sb[:]))
+        d_codes = keep.tile([P, H], U32, name="d_codes", align_bytes=64)
+        nc.vector.tensor_copy(
+            d_codes[:].rearrange("p (t b m) -> p b t m", t=PACK, m=4),
+            d_picked[:].rearrange("p (b m t) -> p b t m", t=PACK, m=4),
+        )
+        x_codes = keep.tile([P, S], U32, name="x_codes", align_bytes=64)
+        nc.vector.tensor_copy(x_codes[:], x_win[:].indirect(offs_sb[:]))
+
+        d_plane = keep.tile([P, H], U8, name="d_plane", align_bytes=64)
+        h = [keep.tile([P, S], F32, name="h_%d" % t) for t in range(PACK)]
+        for t in range(PACK):
+            cols = slice(P * t, P * (t + 1))
+            nc.vector.tensor_copy(d_plane[:, cols], placed[:, t:H:PACK])
+            acc = psum.tile([P, S], F32, name="acc_h")
+            nc.tensor.matmul_mx(
+                out=acc[:],
+                lhsT=d_codes[:, cols].bitcast(FP8X4),
+                lhsT_scale=d_plane[:, cols],
+                rhs=x_codes[:].bitcast(FP8X4),
+                rhs_scale=placed[:, H:],
+                start=True,
+                stop=True,
+            )
+            nc.vector.tensor_scalar(h[t][:], acc[:], 0.0625, None, ALU.mult)
+
+        pa = [keep.tile([P, W], F32, name="pa_%d" % t) for t in range(PACK)]
+        pb = [keep.tile([P, W], F32, name="pb_%d" % t) for t in range(PACK)]
+        rb = [keep.tile([P, W], F32, name="rb_%d" % t) for t in range(PACK)]
+        dt = [keep.tile([P, S], F32, name="dt_%d" % t) for t in range(PACK)]
+        z = [keep.tile([P, W, PACK], BF16, name="z_%d" % c, align_bytes=64) for c in range(2)]
+
+        def fetch_pb(t):
+            nc.scalar.activation(pb[t][:], h[t][:].indirect(n2_sb[:]), COPY)
+
+        def fetch_pa(t):
+            nc.scalar.activation(pa[t][:], h[t][:].indirect(n1_sb[:]), COPY)
+            nc.vector.tensor_tensor(rb[t][:], pa[t][:], pb[t][:], ALU.subtract)
+
+        def put_pb(t):
+            nc.scalar.activation(dt[t][:].indirect(n1_sb[:]), pb[t][:], COPY)
+
+        def put_rb(t):
+            nc.scalar.activation(dt[t][:].indirect(n2_sb[:]), rb[t][:], COPY)
+
+        def make_z(t, c):
+            cols = slice(W * c, W * (c + 1))
+            other = keep.tile([P, W], F32, name="other_%d_%d" % (t, c))
+            nc.scalar.activation(other[:], dt[t][:].indirect(n3_sb[:, 8 * c : 8 * (c + 1)]), COPY)
+            larger = keep.tile([P, W], F32, name="larger_%d_%d" % (t, c))
+            nc.vector.scalar_tensor_tensor(larger[:], other[:], 0.5, dt[t][:, cols], ALU.mult, ALU.max)
+            nc.vector.tensor_scalar(z[c][:, :, t], larger[:], gain[:, t : t + 1], None, ALU.mult)
+
+        def second_product(c):
+            cols = slice(W * c, W * (c + 1))
+            z_codes = keep.tile([P, W], U32, name="z_codes_%d" % c, align_bytes=64)
+            z_plane = keep.tile([P, W], U8, name="z_plane_%d" % c, align_bytes=64)
+            nc.vector.quantize_mx(
+                out=z_codes[:].bitcast(FP8X4), scales=z_plane[:], in_=z[c][:].rearrange("p j t -> p (j t)")
+            )
+            for u in range(4):
+                acc = psum.tile([P, W], F32, name="acc_h2")
+                nc.tensor.matmul_mx(
+                    out=acc[:],
+                    lhsT=w1_sb[:, 2 * P * u : 2 * P * (u + 1)].bitcast(FP4X4),
+                    lhsT_scale=w1_plane[:, P * u : P * (u + 1)],
+                    rhs=z_codes[:].bitcast(FP8X4),
+                    rhs_scale=z_plane[:],
+                    start=True,
+                    stop=True,
+                )
+                nc.vector.tensor_copy(h2[u][:, cols], acc[:])
+
+        fetch_pb(0)
+        fetch_pa(0)
+        for t in range(1, PACK):
+            fetch_pb(t)
+            put_pb(t - 1)
+            fetch_pa(t)
+            put_rb(t - 1)
+        make_z(0, 0)
+        put_pb(3)
+        make_z(1, 0)
+        put_rb(3)
+        make_z(2, 0)
+        make_z(3, 0)
+        second_product(0)
+        for t in range(PACK):
+            make_z(t, 1)
+        second_product(1)
+
+        page = [keep.tile([P, U], F32, name="page_%d" % u) for u in range(4)]
+        nw = [keep.tile([P, S], F32, name="nw_%d" % u) for u in range(4)]
+
+        def put_h2(u, c):
+            nc.scalar.activation(
+                page[u][:].indirect(n4_sb[:, 8 * c : 8 * (c + 1)]), h2[u][:, W * c : W * (c + 1)], COPY
+            )
+
+        def make_nw(u):
+            partner = keep.tile([P, S], F32, name="partner_%d" % u)
+            nc.scalar.activation(partner[:], h2[u][:].indirect(n6_sb[:]), COPY)
+            nc.vector.tensor_tensor(nw[u][:], h2[u][:, :S], partner[:], ALU.subtract)
+
+        def put_nw(u):
+            nc.scalar.activation(page[u][:].indirect(n5_sb[:]), nw[u][:], COPY)
+            nc.sync.dma_start(out[P * u : P * (u + 1), :], page[u][:])
+
+        for u in range(4):
+            put_h2(u, 0)
+        make_nw(0)
+        put_h2(0, 1)
+        for u in range(1, 4):
+            make_nw(u)
+            put_h2(u, 1)
+            put_nw(u - 1)
+        put_nw(3)

@@ -38,19 +38,21 @@ def tile_picked_pqlayswapdpagq_none_p_kernel(
             nc.sync.dma_start(tile[:], src)
             return tile
 
-        d_scale_win = keep.tile([P, T], U8, name="d_scale_win", align_bytes=64)
-        x_scale_win = keep.tile([P, T], U8, name="x_scale_win", tag="shared", align_bytes=64)
-        placed = keep.tile([P, H + S], U8, name="placed", align_bytes=64)
+        d_scale_win = keep.tile([P, T], U8, name="d_scale_win", tag="shared", align_bytes=64)
+        x_scale_win = keep.tile([P, T], U8, name="x_scale_win", align_bytes=64)
+        placed = keep.tile([P, H], U8, name="placed", align_bytes=64)
+        x_plane = keep.tile([P, S], U8, name="x_plane", align_bytes=64)
         w1_plane = keep.tile([P, H], U8, name="w1_plane", align_bytes=64)
-        nc.vector.memset(d_scale_win[:].bitcast(I32), 0)
-        nc.vector.memset(x_scale_win[:].bitcast(I32), 0)
+        nc.gpsimd.memset(d_scale_win[:].bitcast(I32), 0)
+        nc.vector.memset(x_scale_win[:].bitcast(I32)[0:112, :], 0)
+        nc.vector.memset(x_plane[:].bitcast(I32), 0)
         nc.vector.memset(placed[:].bitcast(I32), 0)
         nc.vector.memset(w1_plane[:].bitcast(I32), 0)
 
         k1_sb = load_list(k1, "k1_sb")
         offs_sb = load_list(offs, "offs_sb")
         nc.scalar.dma_start(d_scale_win[:].bitcast(I32)[0:P:8, :], d_scales[0].bitcast(I32))
-        nc.scalar.dma_start(x_scale_win[:].bitcast(I32)[0:P:8, :], x_scales[0].bitcast(I32))
+        nc.scalar.dma_start(x_scale_win[:].bitcast(I32)[112:P, :], x_scales[0].bitcast(I32))
         d_win = keep.tile([P, T], U32, name="d_win", align_bytes=64)
         x_win = keep.tile([P, T], U32, name="x_win", align_bytes=64)
         nc.sync.dma_start(d_win[:].bitcast(I32), d_words[0].rearrange("p n t -> p (n t)").bitcast(I32))
@@ -75,11 +77,17 @@ def tile_picked_pqlayswapdpagq_none_p_kernel(
         for u in range(4):
             nc.vector.memset(h2[u][:, S:], 0.0)
 
-        picked = keep.tile([P, H + S], U8, name="picked", align_bytes=64)
-        nc.vector.tensor_copy(picked[:, :H], d_scale_win[:].indirect(k1_sb[:]))
-        nc.vector.tensor_copy(picked[:, H:], x_scale_win[:].indirect(offs_sb[:]))
+        x_picked = keep.tile([P, S], U8, name="x_picked", align_bytes=64)
+        nc.vector.tensor_copy(x_picked[:], x_scale_win[:].indirect(offs_sb[:]))
+        for q in range(4):
+            nc.scalar.dma_start(
+                x_plane[:].bitcast(I32)[32 * q : 32 * q + 4, :],
+                x_picked[:].bitcast(I32)[112 + 4 * q : 116 + 4 * q, :],
+            )
+        picked = keep.tile([P, H], U8, name="picked", align_bytes=64)
+        nc.vector.tensor_copy(picked[:], d_scale_win[:].indirect(k1_sb[:]))
         for a in range(4):
-            nc.scalar.dma_start(placed[:].bitcast(I32)[a:P:32, :], picked[:].bitcast(I32)[8 * a : P : 32, :])
+            nc.sync.dma_start(placed[:].bitcast(I32)[a:P:32, :], picked[:].bitcast(I32)[8 * a : P : 32, :])
 
         d_picked = keep.tile([P, H], U32, name="d_picked", tag="shared", align_bytes=64)
         nc.vector.tensor_copy(d_picked[:], d_win[:].indirect(k1_sb[:]))
@@ -92,7 +100,7 @@ def tile_picked_pqlayswapdpagq_none_p_kernel(
         nc.vector.tensor_copy(x_codes[:], x_win[:].indirect(offs_sb[:]))
 
         d_plane = keep.tile([P, H], U8, name="d_plane", align_bytes=64)
-        h = [keep.tile([P, S], F32, name="h_%d" % t) for t in range(PACK)]
+        h = [keep.tile([P, S], F32, name="h_%d" % t, tag="h_%d" % t) for t in range(PACK)]
         for t in range(PACK):
             cols = slice(P * t, P * (t + 1))
             nc.vector.tensor_copy(d_plane[:, cols], placed[:, t:H:PACK])
@@ -102,17 +110,17 @@ def tile_picked_pqlayswapdpagq_none_p_kernel(
                 lhsT=d_codes[:, cols].bitcast(FP8X4),
                 lhsT_scale=d_plane[:, cols],
                 rhs=x_codes[:].bitcast(FP8X4),
-                rhs_scale=placed[:, H:],
+                rhs_scale=x_plane[:],
                 start=True,
                 stop=True,
             )
             nc.vector.tensor_scalar(h[t][:], acc[:], 0.0625, None, ALU.mult)
 
         pa = [keep.tile([P, W], F32, name="pa_%d" % t) for t in range(PACK)]
-        pb = [keep.tile([P, W], F32, name="pb_%d" % t) for t in range(PACK)]
-        rb = [keep.tile([P, W], F32, name="rb_%d" % t) for t in range(PACK)]
+        pb = [keep.tile([P, W], F32, name="pb_%d" % t, tag="pb_%d" % t) for t in range(PACK)]
+        rb = [keep.tile([P, W], F32, name="rb_%d" % t, tag="rb_%d" % t) for t in range(PACK)]
         dt = [keep.tile([P, S], F32, name="dt_%d" % t) for t in range(PACK)]
-        z = [keep.tile([P, W, PACK], BF16, name="z_%d" % c, align_bytes=64) for c in range(2)]
+        z = [keep.tile([P, W, PACK], BF16, name="z_%d" % c, tag="z_%d" % c, align_bytes=64) for c in range(2)]
 
         def fetch_pb(t):
             nc.scalar.activation(pb[t][:], h[t][:].indirect(n2_sb[:]), COPY)
@@ -127,13 +135,11 @@ def tile_picked_pqlayswapdpagq_none_p_kernel(
         def put_rb(t):
             nc.scalar.activation(dt[t][:].indirect(n2_sb[:]), rb[t][:], COPY)
 
-        def make_z(t, c):
+        def make_z(t, c, other, larger):
             cols = slice(W * c, W * (c + 1))
-            other = keep.tile([P, W], F32, name="other_%d_%d" % (t, c))
-            nc.scalar.activation(other[:], dt[t][:].indirect(n3_sb[:, 8 * c : 8 * (c + 1)]), COPY)
-            larger = keep.tile([P, W], F32, name="larger_%d_%d" % (t, c))
-            nc.vector.scalar_tensor_tensor(larger[:], other[:], 0.5, dt[t][:, cols], ALU.mult, ALU.max)
-            nc.vector.tensor_scalar(z[c][:, :, t], larger[:], gain[:, t : t + 1], None, ALU.mult)
+            nc.scalar.activation(other, dt[t][:].indirect(n3_sb[:, 8 * c : 8 * (c + 1)]), COPY)
+            nc.vector.scalar_tensor_tensor(larger, other, 0.5, dt[t][:, cols], ALU.mult, ALU.max)
+            nc.vector.tensor_scalar(z[c][:, :, t], larger, gain[:, t : t + 1], None, ALU.mult)
 
         def second_product(c):
             cols = slice(W * c, W * (c + 1))
@@ -162,15 +168,23 @@ def tile_picked_pqlayswapdpagq_none_p_kernel(
             put_pb(t - 1)
             fetch_pa(t)
             put_rb(t - 1)
-        make_z(0, 0)
+        early = keep.tile([P, PACK, W], F32, name="early")
+
+        def fresh(name, tag):
+            tile = keep.tile([P, W], F32, name=name, tag=tag)
+            return tile[:]
+
+        make_z(0, 0, fresh("other_0", "other_0"), early[:, 0, :])
         put_pb(3)
-        make_z(1, 0)
+        make_z(1, 0, fresh("other_1", "h_3"), early[:, 1, :])
         put_rb(3)
-        make_z(2, 0)
-        make_z(3, 0)
+        make_z(2, 0, fresh("other_2", "pb_3"), early[:, 2, :])
+        make_z(3, 0, fresh("other_3", "other_3"), early[:, 3, :])
         second_product(0)
+        late = keep.tile([P, PACK, W], F32, name="late", tag="rb_3")
+        late_larger = keep.tile([P, PACK, W], F32, name="late_larger", tag="z_0", align_bytes=64)
         for t in range(PACK):
-            make_z(t, 1)
+            make_z(t, 1, late[:, t, :], late_larger[:, t, :])
         second_product(1)
 
         page = [keep.tile([P, U], F32, name="page_%d" % u) for u in range(4)]

from contextlib import ExitStack

import concourse.mybir as mybir

F32 = mybir.dt.float32
BF16 = mybir.dt.bfloat16
I32 = mybir.dt.int32
U32 = mybir.dt.uint32
U16 = mybir.dt.uint16
U8 = mybir.dt.uint8
FP8X4 = mybir.dt.float8_e4m3fn_x4
FP4X4 = mybir.dt.float4_e2m1fn_x4
ALU = mybir.AluOpType
COPY = mybir.ActivationFunctionType.Copy

P = 128
PACK = 4
T = 2048
S = 256
H = 512
W = 128
U = 512
SPARE = 8
FLOPS = 2 * 512 * 512 * 256 * 2


def tile_picked_pqlayswapdpagq_none_p_kernel(
    tc, x_words, x_scales, d_words, d_scales, gn, w1_words, w1_scales, offs, k1, n1, n2, n3, n4, n5, n6, out
):
    nc = tc.nc
    with ExitStack() as ctx:
        lists = ctx.enter_context(tc.tile_pool(name="lists", bufs=1))
        keep = ctx.enter_context(tc.tile_pool(name="keep", bufs=1))
        psum = ctx.enter_context(tc.psum_pool(name="psum", bufs=4))

        def load_list(src, name):
            tile = lists.tile(list(src.shape), U16, name=name)
            nc.sync.dma_start(tile[:], src)
            return tile

        d_scale_win = keep.tile([P, T], U8, name="d_scale_win", tag="shared", align_bytes=64)
        x_scale_win = keep.tile([P, T], U8, name="x_scale_win", align_bytes=64)
        placed = keep.tile([P, H], U8, name="placed", align_bytes=64)
        x_plane = keep.tile([P, S], U8, name="x_plane", align_bytes=64)
        w1_plane = keep.tile([P, H], U8, name="w1_plane", align_bytes=64)
        nc.gpsimd.memset(d_scale_win[:].bitcast(I32), 0)
        nc.vector.memset(x_scale_win[:].bitcast(I32)[0:112, :], 0)
        nc.vector.memset(x_plane[:].bitcast(I32), 0)
        nc.vector.memset(placed[:].bitcast(I32), 0)
        nc.vector.memset(w1_plane[:].bitcast(I32), 0)

        k1_sb = load_list(k1, "k1_sb")
        offs_sb = load_list(offs, "offs_sb")
        nc.scalar.dma_start(d_scale_win[:].bitcast(I32)[0:P:8, :], d_scales[0].bitcast(I32))
        nc.scalar.dma_start(x_scale_win[:].bitcast(I32)[112:P, :], x_scales[0].bitcast(I32))
        d_win = keep.tile([P, T], U32, name="d_win", align_bytes=64)
        x_win = keep.tile([P, T], U32, name="x_win", align_bytes=64)
        nc.sync.dma_start(d_win[:].bitcast(I32), d_words[0].rearrange("p n t -> p (n t)").bitcast(I32))
        nc.gpsimd.dma_start(x_win[:].bitcast(I32), x_words[0].rearrange("p n t -> p (n t)").bitcast(I32))
        n2_sb = load_list(n2, "n2_sb")
        n1_sb = load_list(n1, "n1_sb")
        n3_sb = load_list(n3, "n3_sb")
        n4_sb = load_list(n4, "n4_sb")
        n6_sb = load_list(n6, "n6_sb")
        n5_sb = load_list(n5, "n5_sb")

        gain = keep.tile([P, PACK], F32, name="gain")
        nc.gpsimd.dma_start(gain[:], gn.rearrange("(p t) o -> p (t o)", t=PACK))
        w1_sb = keep.tile([P, 2 * H], U8, name="w1_sb", align_bytes=64)
        nc.gpsimd.dma_start(w1_sb[:].bitcast(I32), w1_words[0].bitcast(I32))
        for q in range(4):
            nc.gpsimd.dma_start(
                w1_plane[:].bitcast(I32)[32 * q : 32 * q + 4, :], w1_scales[0].bitcast(I32)[4 * q : 4 * q + 4, :]
            )

        h2 = [keep.tile([P, S + SPARE], F32, name="h2_%d" % u) for u in range(4)]
        for u in range(4):
            nc.vector.memset(h2[u][:, S:], 0.0)

        x_picked = keep.tile([P, S], U8, name="x_picked", align_bytes=64)
        nc.vector.tensor_copy(x_picked[:], x_scale_win[:].indirect(offs_sb[:]))
        for q in range(4):
            nc.scalar.dma_start(
                x_plane[:].bitcast(I32)[32 * q : 32 * q + 4, :],
                x_picked[:].bitcast(I32)[112 + 4 * q : 116 + 4 * q, :],
            )
        picked = keep.tile([P, H], U8, name="picked", align_bytes=64)
        nc.vector.tensor_copy(picked[:], d_scale_win[:].indirect(k1_sb[:]))
        for a in range(4):
            nc.sync.dma_start(placed[:].bitcast(I32)[a:P:32, :], picked[:].bitcast(I32)[8 * a : P : 32, :])

        d_picked = keep.tile([P, H], U32, name="d_picked", tag="shared", align_bytes=64)
        nc.vector.tensor_copy(d_picked[:], d_win[:].indirect(k1_sb[:]))
        d_codes = keep.tile([P, H], U32, name="d_codes", align_bytes=64)
        nc.vector.tensor_copy(
            d_codes[:].rearrange("p (t b m) -> p b t m", t=PACK, m=4),
            d_picked[:].rearrange("p (b m t) -> p b t m", t=PACK, m=4),
        )
        x_codes = keep.tile([P, S], U32, name="x_codes", align_bytes=64)
        nc.vector.tensor_copy(x_codes[:], x_win[:].indirect(offs_sb[:]))

        d_plane = keep.tile([P, H], U8, name="d_plane", align_bytes=64)
        h = [keep.tile([P, S], F32, name="h_%d" % t, tag="h_%d" % t) for t in range(PACK)]
        for t in range(PACK):
            cols = slice(P * t, P * (t + 1))
            nc.vector.tensor_copy(d_plane[:, cols], placed[:, t:H:PACK])
            acc = psum.tile([P, S], F32, name="acc_h")
            nc.tensor.matmul_mx(
                out=acc[:],
                lhsT=d_codes[:, cols].bitcast(FP8X4),
                lhsT_scale=d_plane[:, cols],
                rhs=x_codes[:].bitcast(FP8X4),
                rhs_scale=x_plane[:],
                start=True,
                stop=True,
            )
            nc.vector.tensor_scalar(h[t][:], acc[:], 0.0625, None, ALU.mult)

        pa = [keep.tile([P, W], F32, name="pa_%d" % t) for t in range(PACK)]
        pb = [keep.tile([P, W], F32, name="pb_%d" % t, tag="pb_%d" % t) for t in range(PACK)]
        rb = [keep.tile([P, W], F32, name="rb_%d" % t, tag="rb_%d" % t) for t in range(PACK)]
        dt = [keep.tile([P, S], F32, name="dt_%d" % t) for t in range(PACK)]
        z = [keep.tile([P, W, PACK], BF16, name="z_%d" % c, tag="z_%d" % c, align_bytes=64) for c in range(2)]

        def fetch_pb(t):
            nc.scalar.activation(pb[t][:], h[t][:].indirect(n2_sb[:]), COPY)

        def fetch_pa(t):
            nc.scalar.activation(pa[t][:], h[t][:].indirect(n1_sb[:]), COPY)
            nc.vector.tensor_tensor(rb[t][:], pa[t][:], pb[t][:], ALU.subtract)

        def put_pb(t):
            nc.scalar.activation(dt[t][:].indirect(n1_sb[:]), pb[t][:], COPY)

        def put_rb(t):
            nc.scalar.activation(dt[t][:].indirect(n2_sb[:]), rb[t][:], COPY)

        def make_z(t, c, other, larger):
            cols = slice(W * c, W * (c + 1))
            nc.scalar.activation(other, dt[t][:].indirect(n3_sb[:, 8 * c : 8 * (c + 1)]), COPY)
            nc.vector.scalar_tensor_tensor(larger, other, 0.5, dt[t][:, cols], ALU.mult, ALU.max)
            nc.vector.tensor_scalar(z[c][:, :, t], larger, gain[:, t : t + 1], None, ALU.mult)

        def second_product(c):
            cols = slice(W * c, W * (c + 1))
            z_codes = keep.tile([P, W], U32, name="z_codes_%d" % c, align_bytes=64)
            z_plane = keep.tile([P, W], U8, name="z_plane_%d" % c, align_bytes=64)
            nc.vector.quantize_mx(
                out=z_codes[:].bitcast(FP8X4), scales=z_plane[:], in_=z[c][:].rearrange("p j t -> p (j t)")
            )
            for u in range(4):
                acc = psum.tile([P, W], F32, name="acc_h2")
                nc.tensor.matmul_mx(
                    out=acc[:],
                    lhsT=w1_sb[:, 2 * P * u : 2 * P * (u + 1)].bitcast(FP4X4),
                    lhsT_scale=w1_plane[:, P * u : P * (u + 1)],
                    rhs=z_codes[:].bitcast(FP8X4),
                    rhs_scale=z_plane[:],
                    start=True,
                    stop=True,
                )
                nc.vector.tensor_copy(h2[u][:, cols], acc[:])

        fetch_pb(0)
        fetch_pa(0)
        for t in range(1, PACK):
            fetch_pb(t)
            put_pb(t - 1)
            fetch_pa(t)
            put_rb(t - 1)
        early = keep.tile([P, PACK, W], F32, name="early")

        def fresh(name, tag):
            tile = keep.tile([P, W], F32, name=name, tag=tag)
            return tile[:]

        make_z(0, 0, fresh("other_0", "other_0"), early[:, 0, :])
        put_pb(3)
        make_z(1, 0, fresh("other_1", "h_3"), early[:, 1, :])
        put_rb(3)
        make_z(2, 0, fresh("other_2", "pb_3"), early[:, 2, :])
        make_z(3, 0, fresh("other_3", "other_3"), early[:, 3, :])
        second_product(0)
        late = keep.tile([P, PACK, W], F32, name="late", tag="rb_3")
        late_larger = keep.tile([P, PACK, W], F32, name="late_larger", tag="z_0", align_bytes=64)
        for t in range(PACK):
            make_z(t, 1, late[:, t, :], late_larger[:, t, :])
        second_product(1)

        page = [keep.tile([P, U], F32, name="page_%d" % u) for u in range(4)]
        nw = [keep.tile([P, S], F32, name="nw_%d" % u) for u in range(4)]

        def put_h2(u, c):
            nc.scalar.activation(
                page[u][:].indirect(n4_sb[:, 8 * c : 8 * (c + 1)]), h2[u][:, W * c : W * (c + 1)], COPY
            )

        def make_nw(u):
            partner = keep.tile([P, S], F32, name="partner_%d" % u)
            nc.scalar.activation(partner[:], h2[u][:].indirect(n6_sb[:]), COPY)
            nc.vector.tensor_tensor(nw[u][:], h2[u][:, :S], partner[:], ALU.subtract)

        def put_nw(u):
            nc.scalar.activation(page[u][:].indirect(n5_sb[:]), nw[u][:], COPY)
            nc.sync.dma_start(out[P * u : P * (u + 1), :], page[u][:])

        for u in range(4):
            put_h2(u, 0)
        make_nw(0)
        put_h2(0, 1)
        for u in range(1, 4):
            make_nw(u)
            put_h2(u, 1)
            put_nw(u - 1)
        put_nw(3)
